import numpy as np
import ml_dtypes

BF16 = ml_dtypes.bfloat16


def bf(x):
    return np.asarray(x, np.float32).astype(BF16)


def f32(x):
    return np.asarray(x, np.float32)


def f64(x):
    return np.asarray(x).astype(np.float64)


def striped(idx):
    return np.concatenate([l.reshape(-1, 16).T for l in idx])


def rows(idx, k):
    return np.tile(np.repeat(idx, 16, axis=0), (k // (16 * 8), 1))


def look(tab, idx):
    return np.take_along_axis(f64(tab), rows(idx, len(tab)), axis=1)


P, K, S, V, N = 128, 512, 2048, 1536, 1536


def setup_inputs():
    return {"tab": f32(0.5 * np.random.standard_normal((K, S))), "u": f32(0.3 * np.random.standard_normal((K, V))), "e": bf(np.tile(np.eye(16), (8, 1))), "offs": striped(np.random.randint(0, S, (8, N)))}


def reference(tab, u, e, offs):
    idx = np.stack([g.T.reshape(-1) for g in np.split(offs, 8)])
    s = look(tab, idx) + f64(u)
    s = np.concatenate([f64(e).T @ s[a:a + P] for a in range(0, K, P)])
    x = s
    return x

@@ -1,0 +1,43 @@
+import concourse.mybir as mybir
+
+P, K, S, V, QUERIES = 128, 512, 2048, 1536, 16
+PIECE = 512
+BLOCKS, PIECES = K // P, V // PIECE
+FLOPS = K * V + 2 * K * QUERIES * V
+
+F32, BF16, U16 = mybir.dt.float32, mybir.dt.bfloat16, mybir.dt.uint16
+
+
+def tile_lookup_adc_sum_out_kernel(tc, tab, u, e, offs, out):
+    nc = tc.nc
+    add = mybir.AluOpType.add
+    with (
+        tc.tile_pool(name="held", bufs=1) as held,
+        tc.tile_pool(name="loads", bufs=BLOCKS) as loads,
+        tc.tile_pool(name="work", bufs=3) as work,
+        tc.psum_pool(name="psum", bufs=4) as psum,
+    ):
+        offsets = held.tile([P, V // 16], U16, name="offsets")
+        nc.sync.dma_start(offsets[:], offs)
+        groups = held.tile([P, QUERIES], BF16, name="groups")
+        nc.scalar.dma_start(groups[:], e)
+
+        for block in range(BLOCKS):
+            rows = slice(block * P, (block + 1) * P)
+            table = loads.tile([P, S], F32, name="table")
+            nc.sync.dma_start(table[:], tab[rows, :])
+            correction = loads.tile([P, V], F32, name="correction")
+            nc.sync.dma_start(correction[:], u[rows, :])
+
+            for piece in range(PIECES):
+                columns = slice(piece * PIECE, (piece + 1) * PIECE)
+                picked = table[:].indirect(offsets[:, piece * PIECE // 16 : (piece + 1) * PIECE // 16])
+                terms = work.tile([P, PIECE], F32, name="terms")
+                nc.vector.tensor_tensor(terms[:], picked, correction[:, columns], add)
+                rounded = work.tile([P, PIECE], BF16, name="rounded")
+                nc.scalar.copy(rounded[:], terms[:])
+                scores = psum.tile([QUERIES, PIECE], F32, name="scores")
+                nc.tensor.matmul(scores[:], groups[:], rounded[:], start=True, stop=True)
+                result = work.tile([QUERIES, PIECE], F32, name="result")
+                nc.scalar.copy(result[:], scores[:])
+                nc.sync.dma_start(out[block * QUERIES : (block + 1) * QUERIES, columns], result[:])

@@ -13,8 +13,10 @@ def tile_lookup_adc_sum_out_kernel(tc, tab, u, e, offs, out):
     add = mybir.AluOpType.add
     with (
         tc.tile_pool(name="held", bufs=1) as held,
-        tc.tile_pool(name="loads", bufs=BLOCKS) as loads,
-        tc.tile_pool(name="work", bufs=3) as work,
+        tc.tile_pool(name="tables", bufs=BLOCKS) as tables,
+        tc.tile_pool(name="corrections", bufs=BLOCKS * PIECES) as corrections,
+        tc.tile_pool(name="work", bufs=4) as work,
+        tc.tile_pool(name="results", bufs=BLOCKS * PIECES) as results,
         tc.psum_pool(name="psum", bufs=4) as psum,
     ):
         offsets = held.tile([P, V // 16], U16, name="offsets")
@@ -22,22 +24,27 @@ def tile_lookup_adc_sum_out_kernel(tc, tab, u, e, offs, out):
         groups = held.tile([P, QUERIES], BF16, name="groups")
         nc.scalar.dma_start(groups[:], e)
 
+        looked_up = []
         for block in range(BLOCKS):
             rows = slice(block * P, (block + 1) * P)
-            table = loads.tile([P, S], F32, name="table")
+            table = tables.tile([P, S], F32, name="table")
             nc.sync.dma_start(table[:], tab[rows, :])
-            correction = loads.tile([P, V], F32, name="correction")
-            nc.sync.dma_start(correction[:], u[rows, :])
-
             for piece in range(PIECES):
-                columns = slice(piece * PIECE, (piece + 1) * PIECE)
+                correction = corrections.tile([P, PIECE], F32, name="correction")
+                nc.sync.dma_start(correction[:], u[rows, piece * PIECE : (piece + 1) * PIECE])
+                looked_up.append((table, correction))
+
+        for block in range(BLOCKS):
+            for piece in range(PIECES):
+                table, correction = looked_up[block * PIECES + piece]
                 picked = table[:].indirect(offsets[:, piece * PIECE // 16 : (piece + 1) * PIECE // 16])
                 terms = work.tile([P, PIECE], F32, name="terms")
-                nc.vector.tensor_tensor(terms[:], picked, correction[:, columns], add)
+                nc.vector.tensor_tensor(terms[:], picked, correction[:], add)
                 rounded = work.tile([P, PIECE], BF16, name="rounded")
                 nc.scalar.copy(rounded[:], terms[:])
                 scores = psum.tile([QUERIES, PIECE], F32, name="scores")
                 nc.tensor.matmul(scores[:], groups[:], rounded[:], start=True, stop=True)
-                result = work.tile([QUERIES, PIECE], F32, name="result")
+                result = results.tile([QUERIES, PIECE], F32, name="result")
                 nc.scalar.copy(result[:], scores[:])
+                columns = slice(piece * PIECE, (piece + 1) * PIECE)
                 nc.sync.dma_start(out[block * QUERIES : (block + 1) * QUERIES, columns], result[:])

import concourse.mybir as mybir

P, K, S, V, QUERIES = 128, 512, 2048, 1536, 16
PIECE = 512
BLOCKS, PIECES = K // P, V // PIECE
FLOPS = K * V + 2 * K * QUERIES * V

F32, BF16, U16 = mybir.dt.float32, mybir.dt.bfloat16, mybir.dt.uint16


def tile_lookup_adc_sum_out_kernel(tc, tab, u, e, offs, out):
    nc = tc.nc
    add = mybir.AluOpType.add
    with (
        tc.tile_pool(name="held", bufs=1) as held,
        tc.tile_pool(name="tables", bufs=BLOCKS) as tables,
        tc.tile_pool(name="corrections", bufs=BLOCKS * PIECES) as corrections,
        tc.tile_pool(name="work", bufs=4) as work,
        tc.tile_pool(name="results", bufs=BLOCKS * PIECES) as results,
        tc.psum_pool(name="psum", bufs=4) as psum,
    ):
        offsets = held.tile([P, V // 16], U16, name="offsets")
        nc.sync.dma_start(offsets[:], offs)
        groups = held.tile([P, QUERIES], BF16, name="groups")
        nc.scalar.dma_start(groups[:], e)

        looked_up = []
        for block in range(BLOCKS):
            rows = slice(block * P, (block + 1) * P)
            table = tables.tile([P, S], F32, name="table")
            nc.sync.dma_start(table[:], tab[rows, :])
            for piece in range(PIECES):
                correction = corrections.tile([P, PIECE], F32, name="correction")
                nc.sync.dma_start(correction[:], u[rows, piece * PIECE : (piece + 1) * PIECE])
                looked_up.append((table, correction))

        for block in range(BLOCKS):
            for piece in range(PIECES):
                table, correction = looked_up[block * PIECES + piece]
                picked = table[:].indirect(offsets[:, piece * PIECE // 16 : (piece + 1) * PIECE // 16])
                terms = work.tile([P, PIECE], F32, name="terms")
                nc.vector.tensor_tensor(terms[:], picked, correction[:], add)
                rounded = work.tile([P, PIECE], BF16, name="rounded")
                nc.scalar.copy(rounded[:], terms[:])
                scores = psum.tile([QUERIES, PIECE], F32, name="scores")
                nc.tensor.matmul(scores[:], groups[:], rounded[:], start=True, stop=True)
                result = results.tile([QUERIES, PIECE], F32, name="result")
                nc.scalar.copy(result[:], scores[:])
                columns = slice(piece * PIECE, (piece + 1) * PIECE)
                nc.sync.dma_start(out[block * QUERIES : (block + 1) * QUERIES, columns], result[:])
